import numpy as np
import ml_dtypes


def mxq(x, axis, fmt="e4m3"):
    dtype, down = {"e4m3": (ml_dtypes.float8_e4m3fn, 7), "e5m2": (ml_dtypes.float8_e5m2, 14)}[fmt]
    v = np.moveaxis(np.asarray(x, np.float32).astype(ml_dtypes.bfloat16).astype(np.float64), axis, -1)
    blocks = v.reshape(v.shape[:-1] + (-1, 32))
    amax = np.abs(blocks).max(-1, keepdims=True)
    byte = np.maximum(np.where(amax > 0, np.frexp(amax)[1] - 1 + 127, 0) - down, 1)
    scale = np.exp2(byte - 127.0)
    codes = (blocks / scale).astype(np.float32).astype(dtype).astype(np.float64)
    return np.moveaxis((codes * scale).reshape(v.shape), -1, axis)


WIDE = False


def mx_kscale(k, group=512):
    if not WIDE:
        return np.ones(k)
    levels = np.array([10, -10, 5, -5, 0])
    if group != 512:
        return np.exp2(np.random.permutation(np.resize(levels, k // group))).repeat(group)
    if k % 512:
        return np.exp2(np.random.permutation(np.resize(levels, k // 32))).repeat(32)
    a = np.empty((k // 512, 16))
    for p in range(k // 512):
        a[p, :8] = np.random.permutation(np.resize(levels, 8))
        for g in range(8):
            far = levels[np.abs(levels - a[p, g]) >= 10]
            a[p, g + 8] = far[np.random.randint(len(far))]
    return np.exp2(a.ravel()).repeat(32)


def f64(x):
    return np.asarray(x).astype(np.float64)


E2M1 = np.array([0.0, 0.5, 1.0, 1.5, 2.0, 3.0, 4.0, 6.0, -0.0, -0.5, -1.0, -1.5, -2.0, -3.0, -4.0, -6.0])


def pack_group(w):
    k, n = w.shape
    w = f64(np.asarray(w, np.float32).astype(ml_dtypes.bfloat16)).reshape(k // 32, 32, n)
    amax = np.abs(w).max(1)
    mant, ex = np.frexp(amax / 6.0)
    byte = np.clip(np.where(amax > 0, np.where(mant > 0.5, ex, ex - 1) + 127, 1), 1, 254)
    scaled = (w * np.exp2(127.0 - byte)[:, None, :]).reshape(k, n).astype(np.float32)
    c = np.ascontiguousarray(scaled.reshape(k // 4, 4, n).transpose(0, 2, 1)).astype(ml_dtypes.float4_e2m1fn).view(np.uint8) & 0xF
    return np.ascontiguousarray((c[..., 0::2] | (c[..., 1::2] << 4)).reshape(k // 4, 2 * n)), byte.astype(np.uint8)


def unpack_group(words, scales):
    p, n = words.shape[0], scales.shape[1]
    words = np.ascontiguousarray(words).reshape(p, n, 2)
    nib = np.empty((p, n, 4), np.uint8)
    nib[..., 0::2] = words & 0xF
    nib[..., 1::2] = words >> 4
    return E2M1[nib].transpose(0, 2, 1).reshape(4 * p, n) * np.repeat(np.exp2(scales.astype(np.float64) - 127.0), 32, axis=0)


def gelu(v):
    return 0.5 * v * (1.0 + np.tanh(0.7978845608028654 * (v + 0.044715 * v ** 3)))


G, D, M, N = 4, 256, 128, 1024


def setup_inputs():
    n = np.random.standard_normal
    s = mx_kscale(D, 0)[:, None]
    w_ = [pack_group(w) for w in n((G, D, M)) / np.sqrt(D) / s]
    u_ = [pack_group(w) for w in n((G, D, M)) / np.sqrt(D) / s]
    return {
        "x": (n((G, D, N)) * s).astype(np.float32),
        "w_words": np.stack([w[0] for w in w_]),
        "w_scales": np.stack([w[1] for w in w_]),
        "u_words": np.stack([w[0] for w in u_]),
        "u_scales": np.stack([w[1] for w in u_]),
        "b": (0.5 * n((G, M, 1))).astype(np.float32),
    }


def reference(x, w_words, w_scales, u_words, u_scales, b):
    xq = mxq(f64(x), 1, "e4m3")
    h = np.stack([unpack_group(w_words[g], w_scales[g]) for g in range(G)]).transpose(0, 2, 1) @ xq
    g = np.stack([unpack_group(u_words[g], u_scales[g]) for g in range(G)]).transpose(0, 2, 1) @ xq
    h = h + f64(b)
    y = gelu(h) * g
    return y

@@ -1,0 +1,144 @@
+from contextlib import ExitStack
+
+import concourse.mybir as mybir
+
+G, D, M, N = 4, 256, 128, 1024
+FLOPS = 2 * 2 * G * D * M * N
+
+F32 = mybir.dt.float32
+BF16 = mybir.dt.bfloat16
+I32 = mybir.dt.int32
+U32 = mybir.dt.uint32
+U8 = mybir.dt.uint8
+FP8X4 = mybir.dt.float8_e4m3fn_x4
+FP4X4 = mybir.dt.float4_e2m1fn_x4
+GELU = mybir.ActivationFunctionType.Gelu_apprx_tanh
+MULT = mybir.AluOpType.mult
+
+P = 128
+PACK = 4
+ROWS = D // PACK
+SIDE = P // ROWS
+PAIRS = G // SIDE
+QUAD = 32
+N_TILE = 512
+HALVES = N // N_TILE
+RUN = 4
+VECTOR_COLS = [320,256,256,320]
+
+
+def tile_rows_gglu_gelu_bias_kernel(tc, x, w_words, w_scales, u_words, u_scales, b, out):
+    nc = tc.nc
+    chunks = [(pair, half) for pair in range(PAIRS) for half in range(HALVES)]
+
+    with ExitStack() as ctx:
+        keep = ctx.enter_context(tc.tile_pool(name="keep", bufs=1))
+        psum = ctx.enter_context(tc.psum_pool(name="psum", bufs=1))
+        ctx.enter_context(tc.manual_schedule())
+
+        w_codes = keep.tile([P, PAIRS, 2 * M], U8, align_bytes=64)
+        u_codes = keep.tile([P, PAIRS, 2 * M], U8, align_bytes=64)
+        w_plane = keep.tile([P, PAIRS, M], U8, align_bytes=64)
+        u_plane = keep.tile([P, PAIRS, M], U8, align_bytes=64)
+        b_rows = keep.tile([P, P], F32, align_bytes=64)
+        b_cols = keep.tile([P, P], F32, align_bytes=64)
+        raw = [keep.tile([P, PACK, N_TILE], F32, name="raw%d" % k, align_bytes=64) for k in range(len(chunks))]
+        packed = [keep.tile([P, N_TILE * PACK], BF16, name="packed%d" % k, align_bytes=64) for k in range(len(chunks))]
+        x_codes = [keep.tile([P, N_TILE], U32, name="x_codes%d" % k, align_bytes=64) for k in range(len(chunks))]
+        x_plane = [keep.tile([P, N_TILE], U8, name="x_plane%d" % k, align_bytes=64) for k in range(len(chunks))]
+        act = [keep.tile([P, N], F32, name="act%d" % g, align_bytes=64) for g in range(G)]
+        res = [keep.tile([P, N], F32, name="res%d" % g, align_bytes=64) for g in range(G)]
+        z_bank = [[psum.tile([M, N_TILE], F32, name="z%d%d" % (c, h)) for h in range(HALVES)] for c in range(SIDE)]
+        gate_bank = [[psum.tile([M, N_TILE], F32, name="gate%d%d" % (c, h)) for h in range(HALVES)] for c in range(SIDE)]
+
+        x_rows = x.rearrange("(i c) (p j) n -> i (c p) j n", c=SIDE, j=PACK)
+
+        def load_x(k):
+            pair, half = chunks[k]
+            nc.sync.dma_start(out=raw[k][:], in_=x_rows[pair, :, :, half * N_TILE : (half + 1) * N_TILE])
+
+        def load_words(tile, words):
+            src = words.rearrange("(i c) p w -> (c p) i w", c=SIDE)
+            nc.sync.dma_start(out=tile[:].bitcast(I32), in_=src.bitcast(I32))
+
+        def load_scales(queue, tile, scales):
+            src = scales.rearrange("(i c) (s r) m -> (c s) r i m", c=SIDE, r=4)
+            for q in range(P // QUAD):
+                queue.dma_start(out=tile[QUAD * q : QUAD * q + 4, :, :].bitcast(I32), in_=src[q].bitcast(I32))
+
+        def interleave(k):
+            split = VECTOR_COLS[k]
+            for lo, hi, copy in ((0, split, nc.vector.tensor_copy), (split, N_TILE, nc.scalar.copy)):
+                copy(
+                    out=packed[k][:, PACK * lo : PACK * hi].rearrange("p (c i j) -> p c j i", i=RUN, j=PACK),
+                    in_=raw[k][:, :, lo:hi].rearrange("p j (c i) -> p c j i", i=RUN),
+                )
+
+        def quantise(k):
+            nc.vector.quantize_mx(out=x_codes[k][:].bitcast(FP8X4), scales=x_plane[k][:], in_=packed[k][:])
+
+        def multiply(k):
+            pair, half = chunks[k]
+            for banks, codes, plane in ((z_bank, w_codes, w_plane), (gate_bank, u_codes, u_plane)):
+                for c in range(SIDE):
+                    rows = slice(ROWS * c, ROWS * (c + 1))
+                    nc.tensor.matmul_mx(
+                        out=banks[c][half][:],
+                        lhsT=codes[rows, pair, :].bitcast(FP4X4),
+                        lhsT_scale=plane[rows, pair, :],
+                        rhs=x_codes[k][rows, :].bitcast(FP8X4),
+                        rhs_scale=x_plane[k][rows, :],
+                        start=True,
+                        stop=True,
+                    )
+
+        def activate(k):
+            pair, half = chunks[k]
+            cols = slice(half * N_TILE, (half + 1) * N_TILE)
+            for c in range(SIDE):
+                g = SIDE * pair + c
+                nc.scalar.activation(
+                    out=act[g][:, cols], in_=z_bank[c][half][:], func=GELU, bias=b_cols[:, QUAD * g : QUAD * g + 1]
+                )
+
+        def gate(k):
+            pair, half = chunks[k]
+            cols = slice(half * N_TILE, (half + 1) * N_TILE)
+            for c in range(SIDE):
+                g = SIDE * pair + c
+                nc.vector.tensor_tensor(out=res[g][:, cols], in0=act[g][:, cols], in1=gate_bank[c][half][:], op=MULT)
+
+        def store(g, cols):
+            nc.sync.dma_start(out=out[g, :, cols], in_=res[g][:, cols])
+
+        nc.vector.memset(u_plane[:].bitcast(I32), 0)
+        nc.vector.memset(w_plane[:].bitcast(I32), 0)
+        nc.vector.memset(b_rows[:], 0.0)
+
+        load_x(0)
+        load_words(w_codes, w_words)
+        load_words(u_codes, u_words)
+        load_scales(nc.sync, w_plane, w_scales)
+        for k in range(1, len(chunks)):
+            load_x(k)
+        nc.gpsimd.dma_start(
+            out=b_rows[0:P:QUAD, :].rearrange("q (g r) -> q g r", r=QUAD),
+            in_=b.rearrange("g (q r) o -> q g (r o)", r=QUAD),
+        )
+        load_scales(nc.gpsimd, u_plane, u_scales)
+        nc.vector.transpose(out=b_cols[:], in_=b_rows[:])
+
+        for k in range(len(chunks) + 1):
+            if k < len(chunks):
+                interleave(k)
+                quantise(k)
+                multiply(k)
+            if k > 0:
+                activate(k - 1)
+                gate(k - 1)
+
+        for g in range(SIDE):
+            store(g, slice(0, N))
+        for half in range(HALVES):
+            for g in range(SIDE, G):
+                store(g, slice(half * N_TILE, (half + 1) * N_TILE))

@@ -42,6 +42,7 @@ def tile_rows_gglu_gelu_bias_kernel(tc, x, w_words, w_scales, u_words, u_scales,
         u_plane = keep.tile([P, PAIRS, M], U8, align_bytes=64)
         b_rows = keep.tile([P, P], F32, align_bytes=64)
         b_cols = keep.tile([P, P], F32, align_bytes=64)
+        warm = keep.tile([P, 16], F32, align_bytes=64)
         raw = [keep.tile([P, PACK, N_TILE], F32, name="raw%d" % k, align_bytes=64) for k in range(len(chunks))]
         packed = [keep.tile([P, N_TILE * PACK], BF16, name="packed%d" % k, align_bytes=64) for k in range(len(chunks))]
         x_codes = [keep.tile([P, N_TILE], U32, name="x_codes%d" % k, align_bytes=64) for k in range(len(chunks))]
@@ -101,44 +102,51 @@ def tile_rows_gglu_gelu_bias_kernel(tc, x, w_words, w_scales, u_words, u_scales,
                     out=act[g][:, cols], in_=z_bank[c][half][:], func=GELU, bias=b_cols[:, QUAD * g : QUAD * g + 1]
                 )
 
-        def gate(k):
+        def gate(k, c):
             pair, half = chunks[k]
             cols = slice(half * N_TILE, (half + 1) * N_TILE)
-            for c in range(SIDE):
-                g = SIDE * pair + c
-                nc.vector.tensor_tensor(out=res[g][:, cols], in0=act[g][:, cols], in1=gate_bank[c][half][:], op=MULT)
+            g = SIDE * pair + c
+            nc.vector.tensor_tensor(out=res[g][:, cols], in0=act[g][:, cols], in1=gate_bank[c][half][:], op=MULT)
 
         def store(g, cols):
             nc.sync.dma_start(out=out[g, :, cols], in_=res[g][:, cols])
 
-        nc.vector.memset(u_plane[:].bitcast(I32), 0)
         nc.vector.memset(w_plane[:].bitcast(I32), 0)
+        nc.vector.memset(warm[:, 0:1], 0.0)
+        nc.scalar.activation(out=warm[:, 8:9], in_=warm[:, 0:1], func=GELU)
         nc.vector.memset(b_rows[:], 0.0)
+        nc.vector.memset(u_plane[:].bitcast(I32), 0)
 
         load_x(0)
         load_words(w_codes, w_words)
-        load_words(u_codes, u_words)
         load_scales(nc.sync, w_plane, w_scales)
-        for k in range(1, len(chunks)):
-            load_x(k)
-        nc.gpsimd.dma_start(
+        nc.sync.dma_start(
             out=b_rows[0:P:QUAD, :].rearrange("q (g r) -> q g r", r=QUAD),
             in_=b.rearrange("g (q r) o -> q g (r o)", r=QUAD),
         )
-        load_scales(nc.gpsimd, u_plane, u_scales)
-        nc.vector.transpose(out=b_cols[:], in_=b_rows[:])
+        load_x(1)
+        load_words(u_codes, u_words)
+        load_scales(nc.sync, u_plane, u_scales)
+        load_x(2)
+        load_x(3)
 
-        for k in range(len(chunks) + 1):
-            if k < len(chunks):
-                interleave(k)
-                quantise(k)
-                multiply(k)
-            if k > 0:
+        last = len(chunks) - 1
+        for k in range(len(chunks)):
+            interleave(k)
+            if k == 0:
+                nc.vector.transpose(out=b_cols[:], in_=b_rows[:])
+            if k >= 2:
+                gate(k - 2, 1)
+            quantise(k)
+            multiply(k)
+            if k >= 1:
                 activate(k - 1)
-                gate(k - 1)
+                gate(k - 1, 0)
+        gate(last - 1, 1)
+        activate(last)
+        gate(last, 0)
+        gate(last, 1)
 
-        for g in range(SIDE):
-            store(g, slice(0, N))
-        for half in range(HALVES):
-            for g in range(SIDE, G):
-                store(g, slice(half * N_TILE, (half + 1) * N_TILE))
+        for pair, half in chunks:
+            for c in range(SIDE):
+                store(SIDE * pair + c, slice(half * N_TILE, (half + 1) * N_TILE))

@@ -23,8 +23,8 @@ PAIRS = G // SIDE
 QUAD = 32
 N_TILE = 512
 HALVES = N // N_TILE
-RUN = 4
-VECTOR_COLS = [320,256,256,320]
+RUN = 2
+VECTOR_COLS = [352, 288, 288, 336]
 
 
 def tile_rows_gglu_gelu_bias_kernel(tc, x, w_words, w_scales, u_words, u_scales, b, out):
@@ -135,9 +135,11 @@ def tile_rows_gglu_gelu_bias_kernel(tc, x, w_words, w_scales, u_words, u_scales,
             interleave(k)
             if k == 0:
                 nc.vector.transpose(out=b_cols[:], in_=b_rows[:])
-            if k >= 2:
+            if 2 <= k < last:
                 gate(k - 2, 1)
             quantise(k)
+            if k == last:
+                gate(k - 2, 1)
             multiply(k)
             if k >= 1:
                 activate(k - 1)

@@ -24,7 +24,7 @@ QUAD = 32
 N_TILE = 512
 HALVES = N // N_TILE
 RUN = 2
-VECTOR_COLS = [352, 288, 288, 336]
+PIECES = [(0, 0, 512, 352), (1, 0, 512, 288), (2, 0, 512, 272), (3, 0, 256, 112), (3, 256, 512, 160)]
 
 
 def tile_rows_gglu_gelu_bias_kernel(tc, x, w_words, w_scales, u_words, u_scales, b, out):
@@ -43,7 +43,9 @@ def tile_rows_gglu_gelu_bias_kernel(tc, x, w_words, w_scales, u_words, u_scales,
         b_rows = keep.tile([P, P], F32, align_bytes=64)
         b_cols = keep.tile([P, P], F32, align_bytes=64)
         warm = keep.tile([P, 16], F32, align_bytes=64)
-        raw = [keep.tile([P, PACK, N_TILE], F32, name="raw%d" % k, align_bytes=64) for k in range(len(chunks))]
+        raw = [
+            keep.tile([P, PACK, hi - lo], F32, name="raw%d" % i, align_bytes=64) for i, (k, lo, hi, share) in enumerate(PIECES)
+        ]
         packed = [keep.tile([P, N_TILE * PACK], BF16, name="packed%d" % k, align_bytes=64) for k in range(len(chunks))]
         x_codes = [keep.tile([P, N_TILE], U32, name="x_codes%d" % k, align_bytes=64) for k in range(len(chunks))]
         x_plane = [keep.tile([P, N_TILE], U8, name="x_plane%d" % k, align_bytes=64) for k in range(len(chunks))]
@@ -54,9 +56,10 @@ def tile_rows_gglu_gelu_bias_kernel(tc, x, w_words, w_scales, u_words, u_scales,
 
         x_rows = x.rearrange("(i c) (p j) n -> i (c p) j n", c=SIDE, j=PACK)
 
-        def load_x(k):
+        def load_x(i):
+            k, lo, hi, share = PIECES[i]
             pair, half = chunks[k]
-            nc.sync.dma_start(out=raw[k][:], in_=x_rows[pair, :, :, half * N_TILE : (half + 1) * N_TILE])
+            nc.sync.dma_start(out=raw[i][:], in_=x_rows[pair, :, :, half * N_TILE + lo : half * N_TILE + hi])
 
         def load_words(tile, words):
             src = words.rearrange("(i c) p w -> (c p) i w", c=SIDE)
@@ -67,16 +70,19 @@ def tile_rows_gglu_gelu_bias_kernel(tc, x, w_words, w_scales, u_words, u_scales,
             for q in range(P // QUAD):
                 queue.dma_start(out=tile[QUAD * q : QUAD * q + 4, :, :].bitcast(I32), in_=src[q].bitcast(I32))
 
-        def interleave(k):
-            split = VECTOR_COLS[k]
-            for lo, hi, copy in ((0, split, nc.vector.tensor_copy), (split, N_TILE, nc.scalar.copy)):
+        def interleave(i):
+            k, lo, hi, share = PIECES[i]
+            for first, end, copy in ((0, share, nc.vector.tensor_copy), (share, hi - lo, nc.scalar.copy)):
                 copy(
-                    out=packed[k][:, PACK * lo : PACK * hi].rearrange("p (c i j) -> p c j i", i=RUN, j=PACK),
-                    in_=raw[k][:, :, lo:hi].rearrange("p j (c i) -> p c j i", i=RUN),
+                    out=packed[k][:, PACK * (lo + first) : PACK * (lo + end)].rearrange("p (c i j) -> p c j i", i=RUN, j=PACK),
+                    in_=raw[i][:, :, first:end].rearrange("p j (c i) -> p c j i", i=RUN),
                 )
 
-        def quantise(k):
-            nc.vector.quantize_mx(out=x_codes[k][:].bitcast(FP8X4), scales=x_plane[k][:], in_=packed[k][:])
+        def quantise(i):
+            k, lo, hi, share = PIECES[i]
+            nc.vector.quantize_mx(
+                out=x_codes[k][:, lo:hi].bitcast(FP8X4), scales=x_plane[k][:, lo:hi], in_=packed[k][:, PACK * lo : PACK * hi]
+            )
 
         def multiply(k):
             pair, half = chunks[k]
@@ -93,14 +99,13 @@ def tile_rows_gglu_gelu_bias_kernel(tc, x, w_words, w_scales, u_words, u_scales,
                         stop=True,
                     )
 
-        def activate(k):
+        def activate(k, c):
             pair, half = chunks[k]
             cols = slice(half * N_TILE, (half + 1) * N_TILE)
-            for c in range(SIDE):
-                g = SIDE * pair + c
-                nc.scalar.activation(
-                    out=act[g][:, cols], in_=z_bank[c][half][:], func=GELU, bias=b_cols[:, QUAD * g : QUAD * g + 1]
-                )
+            g = SIDE * pair + c
+            nc.scalar.activation(
+                out=act[g][:, cols], in_=z_bank[c][half][:], func=GELU, bias=b_cols[:, QUAD * g : QUAD * g + 1]
+            )
 
         def gate(k, c):
             pair, half = chunks[k]
@@ -129,25 +134,39 @@ def tile_rows_gglu_gelu_bias_kernel(tc, x, w_words, w_scales, u_words, u_scales,
         load_scales(nc.sync, u_plane, u_scales)
         load_x(2)
         load_x(3)
+        load_x(4)
 
-        last = len(chunks) - 1
-        for k in range(len(chunks)):
-            interleave(k)
-            if k == 0:
-                nc.vector.transpose(out=b_cols[:], in_=b_rows[:])
-            if 2 <= k < last:
-                gate(k - 2, 1)
-            quantise(k)
-            if k == last:
-                gate(k - 2, 1)
-            multiply(k)
-            if k >= 1:
-                activate(k - 1)
-                gate(k - 1, 0)
-        gate(last - 1, 1)
-        activate(last)
-        gate(last, 0)
-        gate(last, 1)
+        interleave(0)
+        nc.vector.transpose(out=b_cols[:], in_=b_rows[:])
+        quantise(0)
+        multiply(0)
+
+        interleave(1)
+        quantise(1)
+        multiply(1)
+        activate(0, 0)
+        activate(0, 1)
+        gate(0, 0)
+
+        interleave(2)
+        gate(0, 1)
+        quantise(2)
+        multiply(2)
+        activate(1, 0)
+        gate(1, 0)
+
+        interleave(3)
+        activate(1, 1)
+        interleave(4)
+        quantise(3)
+        quantise(4)
+        gate(1, 1)
+        multiply(3)
+
+        for k in (2, 3):
+            for c in range(SIDE):
+                activate(k, c)
+                gate(k, c)
 
         for pair, half in chunks:
             for c in range(SIDE):

from contextlib import ExitStack

import concourse.mybir as mybir

G, D, M, N = 4, 256, 128, 1024
FLOPS = 2 * 2 * G * D * M * N

F32 = mybir.dt.float32
BF16 = mybir.dt.bfloat16
I32 = mybir.dt.int32
U32 = mybir.dt.uint32
U8 = mybir.dt.uint8
FP8X4 = mybir.dt.float8_e4m3fn_x4
FP4X4 = mybir.dt.float4_e2m1fn_x4
GELU = mybir.ActivationFunctionType.Gelu_apprx_tanh
MULT = mybir.AluOpType.mult

P = 128
PACK = 4
ROWS = D // PACK
SIDE = P // ROWS
PAIRS = G // SIDE
QUAD = 32
N_TILE = 512
HALVES = N // N_TILE
RUN = 2
PIECES = [(0, 0, 512, 352), (1, 0, 512, 288), (2, 0, 512, 272), (3, 0, 256, 112), (3, 256, 512, 160)]


def tile_rows_gglu_gelu_bias_kernel(tc, x, w_words, w_scales, u_words, u_scales, b, out):
    nc = tc.nc
    chunks = [(pair, half) for pair in range(PAIRS) for half in range(HALVES)]

    with ExitStack() as ctx:
        keep = ctx.enter_context(tc.tile_pool(name="keep", bufs=1))
        psum = ctx.enter_context(tc.psum_pool(name="psum", bufs=1))
        ctx.enter_context(tc.manual_schedule())

        w_codes = keep.tile([P, PAIRS, 2 * M], U8, align_bytes=64)
        u_codes = keep.tile([P, PAIRS, 2 * M], U8, align_bytes=64)
        w_plane = keep.tile([P, PAIRS, M], U8, align_bytes=64)
        u_plane = keep.tile([P, PAIRS, M], U8, align_bytes=64)
        b_rows = keep.tile([P, P], F32, align_bytes=64)
        b_cols = keep.tile([P, P], F32, align_bytes=64)
        warm = keep.tile([P, 16], F32, align_bytes=64)
        raw = [
            keep.tile([P, PACK, hi - lo], F32, name="raw%d" % i, align_bytes=64) for i, (k, lo, hi, share) in enumerate(PIECES)
        ]
        packed = [keep.tile([P, N_TILE * PACK], BF16, name="packed%d" % k, align_bytes=64) for k in range(len(chunks))]
        x_codes = [keep.tile([P, N_TILE], U32, name="x_codes%d" % k, align_bytes=64) for k in range(len(chunks))]
        x_plane = [keep.tile([P, N_TILE], U8, name="x_plane%d" % k, align_bytes=64) for k in range(len(chunks))]
        act = [keep.tile([P, N], F32, name="act%d" % g, align_bytes=64) for g in range(G)]
        res = [keep.tile([P, N], F32, name="res%d" % g, align_bytes=64) for g in range(G)]
        z_bank = [[psum.tile([M, N_TILE], F32, name="z%d%d" % (c, h)) for h in range(HALVES)] for c in range(SIDE)]
        gate_bank = [[psum.tile([M, N_TILE], F32, name="gate%d%d" % (c, h)) for h in range(HALVES)] for c in range(SIDE)]

        x_rows = x.rearrange("(i c) (p j) n -> i (c p) j n", c=SIDE, j=PACK)

        def load_x(i):
            k, lo, hi, share = PIECES[i]
            pair, half = chunks[k]
            nc.sync.dma_start(out=raw[i][:], in_=x_rows[pair, :, :, half * N_TILE + lo : half * N_TILE + hi])

        def load_words(tile, words):
            src = words.rearrange("(i c) p w -> (c p) i w", c=SIDE)
            nc.sync.dma_start(out=tile[:].bitcast(I32), in_=src.bitcast(I32))

        def load_scales(queue, tile, scales):
            src = scales.rearrange("(i c) (s r) m -> (c s) r i m", c=SIDE, r=4)
            for q in range(P // QUAD):
                queue.dma_start(out=tile[QUAD * q : QUAD * q + 4, :, :].bitcast(I32), in_=src[q].bitcast(I32))

        def interleave(i):
            k, lo, hi, share = PIECES[i]
            for first, end, copy in ((0, share, nc.vector.tensor_copy), (share, hi - lo, nc.scalar.copy)):
                copy(
                    out=packed[k][:, PACK * (lo + first) : PACK * (lo + end)].rearrange("p (c i j) -> p c j i", i=RUN, j=PACK),
                    in_=raw[i][:, :, first:end].rearrange("p j (c i) -> p c j i", i=RUN),
                )

        def quantise(i):
            k, lo, hi, share = PIECES[i]
            nc.vector.quantize_mx(
                out=x_codes[k][:, lo:hi].bitcast(FP8X4), scales=x_plane[k][:, lo:hi], in_=packed[k][:, PACK * lo : PACK * hi]
            )

        def multiply(k):
            pair, half = chunks[k]
            for banks, codes, plane in ((z_bank, w_codes, w_plane), (gate_bank, u_codes, u_plane)):
                for c in range(SIDE):
                    rows = slice(ROWS * c, ROWS * (c + 1))
                    nc.tensor.matmul_mx(
                        out=banks[c][half][:],
                        lhsT=codes[rows, pair, :].bitcast(FP4X4),
                        lhsT_scale=plane[rows, pair, :],
                        rhs=x_codes[k][rows, :].bitcast(FP8X4),
                        rhs_scale=x_plane[k][rows, :],
                        start=True,
                        stop=True,
                    )

        def activate(k, c):
            pair, half = chunks[k]
            cols = slice(half * N_TILE, (half + 1) * N_TILE)
            g = SIDE * pair + c
            nc.scalar.activation(
                out=act[g][:, cols], in_=z_bank[c][half][:], func=GELU, bias=b_cols[:, QUAD * g : QUAD * g + 1]
            )

        def gate(k, c):
            pair, half = chunks[k]
            cols = slice(half * N_TILE, (half + 1) * N_TILE)
            g = SIDE * pair + c
            nc.vector.tensor_tensor(out=res[g][:, cols], in0=act[g][:, cols], in1=gate_bank[c][half][:], op=MULT)

        def store(g, cols):
            nc.sync.dma_start(out=out[g, :, cols], in_=res[g][:, cols])

        nc.vector.memset(w_plane[:].bitcast(I32), 0)
        nc.vector.memset(warm[:, 0:1], 0.0)
        nc.scalar.activation(out=warm[:, 8:9], in_=warm[:, 0:1], func=GELU)
        nc.vector.memset(b_rows[:], 0.0)
        nc.vector.memset(u_plane[:].bitcast(I32), 0)

        load_x(0)
        load_words(w_codes, w_words)
        load_scales(nc.sync, w_plane, w_scales)
        nc.sync.dma_start(
            out=b_rows[0:P:QUAD, :].rearrange("q (g r) -> q g r", r=QUAD),
            in_=b.rearrange("g (q r) o -> q g (r o)", r=QUAD),
        )
        load_x(1)
        load_words(u_codes, u_words)
        load_scales(nc.sync, u_plane, u_scales)
        load_x(2)
        load_x(3)
        load_x(4)

        interleave(0)
        nc.vector.transpose(out=b_cols[:], in_=b_rows[:])
        quantise(0)
        multiply(0)

        interleave(1)
        quantise(1)
        multiply(1)
        activate(0, 0)
        activate(0, 1)
        gate(0, 0)

        interleave(2)
        gate(0, 1)
        quantise(2)
        multiply(2)
        activate(1, 0)
        gate(1, 0)

        interleave(3)
        activate(1, 1)
        interleave(4)
        quantise(3)
        quantise(4)
        gate(1, 1)
        multiply(3)

        for k in (2, 3):
            for c in range(SIDE):
                activate(k, c)
                gate(k, c)

        for pair, half in chunks:
            for c in range(SIDE):
                store(SIDE * pair + c, slice(half * N_TILE, (half + 1) * N_TILE))
